import numpy as np
import ml_dtypes


def mxq(x, axis, fmt="e4m3"):
    dtype, down = {"e4m3": (ml_dtypes.float8_e4m3fn, 7), "e5m2": (ml_dtypes.float8_e5m2, 14)}[fmt]
    v = np.moveaxis(np.asarray(x, np.float32).astype(ml_dtypes.bfloat16).astype(np.float64), axis, -1)
    blocks = v.reshape(v.shape[:-1] + (-1, 32))
    amax = np.abs(blocks).max(-1, keepdims=True)
    byte = np.maximum(np.where(amax > 0, np.frexp(amax)[1] - 1 + 127, 0) - down, 1)
    scale = np.exp2(byte - 127.0)
    codes = (blocks / scale).astype(np.float32).astype(dtype).astype(np.float64)
    return np.moveaxis((codes * scale).reshape(v.shape), -1, axis)


WIDE = False


def mx_kscale(k):
    if not WIDE:
        return np.ones(k)
    levels = np.array([10, -10, 5, -5, 0])
    if k % 512:
        return np.exp2(np.random.permutation(np.resize(levels, k // 32))).repeat(32)
    a = np.empty((k // 512, 16))
    for p in range(k // 512):
        a[p, :8] = np.random.permutation(np.resize(levels, 8))
        for g in range(8):
            far = levels[np.abs(levels - a[p, g]) >= 10]
            a[p, g + 8] = far[np.random.randint(len(far))]
    return np.exp2(a.ravel()).repeat(32)


def f64(x):
    return np.asarray(x).astype(np.float64)


def striped(idx):
    return np.tile(idx.reshape(-1, 16).T, (8, 1)).astype(np.uint16)


def unstriped(offs):
    return offs[:16].T.reshape(-1).astype(np.int64)


def pack_weight(w):
    k, n = w.shape
    w = f64(np.asarray(w, np.float32).astype(ml_dtypes.bfloat16)).reshape(k // 32, 32, n)
    amax = np.abs(w).max(1)
    byte = np.clip(np.where(amax > 0, np.frexp(amax)[1] - 1 + 127 - 7, 1), 1, 254)
    scaled = (w * np.exp2(127.0 - byte)[:, None, :]).reshape(k, n).astype(np.float32)
    words = np.ascontiguousarray(scaled.reshape(k // 512, 128, 4, n).transpose(0, 1, 3, 2)).astype(ml_dtypes.float8_e4m3fn).view(np.uint8)
    return words, np.ascontiguousarray(byte.astype(np.uint8).reshape(k // 512, 16, n))


def unpack_weight(words, scales):
    g, p, n, _ = words.shape
    vals = np.ascontiguousarray(words).view(ml_dtypes.float8_e4m3fn).astype(np.float64) * np.repeat(np.exp2(scales.astype(np.float64) - 127.0), 8, axis=1)[..., None]
    return vals.transpose(0, 1, 3, 2).reshape(g * 512, n)


K, T, S, N, H, U = 512, 2048, 512, 256, 512, 1024


def setup_inputs():
    n = np.random.standard_normal
    s = mx_kscale(K)[:, None]
    u = mx_kscale(H)
    packed_xT = pack_weight(n((K, T)) * s)
    return {
        "x_words": packed_xT[0],
        "x_scales": packed_xT[1],
        "w1": (n((K, H)) / np.sqrt(K) / s).astype(np.float32),
        "w2": (n((K, H)) / np.sqrt(K) / s).astype(np.float32),
        "rad": (np.random.uniform(0.6, 2.5, (H, U))).astype(np.float32),
        "unit": (np.random.uniform(0.6, 1.4, (H, 1)) * u[:, None]).astype(np.float32),
        "w3": (n((H, N)) / np.sqrt(H) / u[:, None]).astype(np.float32),
        "offs": striped(np.random.permutation(T)[:S]),
        "pa": striped(np.random.permutation(np.concatenate([np.arange(S), np.random.randint(0, S, U - S)]))),
        "pb": striped(np.random.permutation(np.concatenate([np.arange(S), np.random.randint(0, S, U - S)]))),
    }


def reference(x_words, x_scales, w1, w2, rad, unit, w3, offs, pa, pb):
    xq = unpack_weight(x_words, x_scales)[:, unstriped(offs)]
    ure = mxq(f64(w1), 0, "e4m3").T @ xq
    ra = ure[:, unstriped(pa)]
    ga = ra / f64(rad)
    uim = mxq(f64(w2), 0, "e4m3").T @ xq
    ib = uim[:, unstriped(pb)]
    gb = ib / (f64(rad) + 0.5)
    pr2 = (ga) ** 2 + (gb) ** 2 + 0.8 * (ga * gb)
    ampl = np.sqrt(pr2 + 0.05)
    hid = f64(unit) * (ampl - (0.5 * ga))
    return mxq(f64(w3), 0, "e4m3").T @ mxq(hid, 0, "e4m3")

@@ -1,0 +1,243 @@
+import math
+from contextlib import ExitStack
+
+import concourse.mybir as mybir
+from concourse.masks import make_identity
+
+K, T, S, N, H, U = 512, 2048, 512, 256, 512, 1024
+FLOPS = 2 * K * H * S * 2 + 2 * H * N * U
+
+F32 = mybir.dt.float32
+BF16 = mybir.dt.bfloat16
+I32 = mybir.dt.int32
+U32 = mybir.dt.uint32
+U16 = mybir.dt.uint16
+U8 = mybir.dt.uint8
+FP8X4 = mybir.dt.float8_e4m3fn_x4
+ALU = mybir.AluOpType
+ACT = mybir.ActivationFunctionType
+
+P = 128
+PACK = 4
+HALF = 512
+GROUP = 256
+LIST_COL = 16
+
+
+def tile_picked_yacoust_amp_p_kernel(tc, x_words, x_scales, w1, w2, rad, unit, w3, offs, pa, pb, out):
+    nc = tc.nc
+    with ExitStack() as ctx:
+        keep = ctx.enter_context(tc.tile_pool(name="keep", bufs=1))
+        ring = ctx.enter_context(tc.tile_pool(name="ring", bufs=3))
+        psum = ctx.enter_context(tc.psum_pool(name="psum", bufs=2))
+
+        offs_sb = keep.tile([P, S // LIST_COL], U16, name="offs_sb")
+        pa_sb = keep.tile([P, U // LIST_COL], U16, name="pa_sb")
+        pb_sb = keep.tile([P, U // LIST_COL], U16, name="pb_sb")
+        xw = keep.tile([P, T], I32, name="xw")
+        xs = keep.tile([P, T], U8, name="xs")
+        w1_raw = keep.tile([P, PACK, H], F32, name="w1_raw")
+        w2_raw = keep.tile([P, PACK, H], F32, name="w2_raw")
+        w3_raw = keep.tile([P, PACK, N], F32, name="w3_raw")
+        unit_sb = keep.tile([P, PACK], F32, name="unit_sb")
+        ident = keep.tile([P, P], F32, name="ident")
+        pieces = [(half, j) for half in range(U // HALF) for j in range(PACK)]
+        rad_sb = {pc: keep.tile([P, HALF], F32, name="rad_%d_%d" % pc, tag="rad_%d_%d" % pc) for pc in pieces}
+        inv_a = {pc: keep.tile([P, HALF], F32, name="inv_a_%d_%d" % pc) for pc in pieces}
+        inv_b = {pc: keep.tile([P, HALF], F32, name="inv_b_%d_%d" % pc) for pc in pieces}
+        rad_rows = rad.rearrange("(p j) r -> p j r", j=PACK)
+
+        def load_rad(pc):
+            half, j = pc
+            nc.sync.dma_start(out=rad_sb[pc][:], in_=rad_rows[:, j, half * HALF : (half + 1) * HALF])
+
+        nc.vector.memset(xs[:].bitcast(I32), 0)
+
+        load_rad(pieces[0])
+        load_rad(pieces[1])
+        nc.sync.dma_start(out=w1_raw[:], in_=w1.rearrange("(p j) c -> p j c", j=PACK))
+        nc.sync.dma_start(offs_sb[:], offs)
+        for q in range(4):
+            nc.sync.dma_start(out=xs[32 * q : 32 * q + 4, :].bitcast(I32), in_=x_scales[0, 4 * q : 4 * q + 4, :].bitcast(I32))
+        make_identity(nc, ident[:])
+        load_rad(pieces[2])
+        nc.sync.dma_start(out=xw[:], in_=x_words[0].rearrange("p n t -> p (n t)").bitcast(I32))
+        nc.sync.dma_start(out=unit_sb[:], in_=unit.rearrange("(p j) o -> p (j o)", j=PACK))
+        nc.sync.dma_start(pa_sb[:], pa)
+        nc.sync.dma_start(pb_sb[:], pb)
+        nc.sync.dma_start(out=w2_raw[:], in_=w2.rearrange("(p j) c -> p j c", j=PACK))
+        load_rad(pieces[3])
+        load_rad(pieces[4])
+        load_rad(pieces[5])
+        load_rad(pieces[6])
+        load_rad(pieces[7])
+        nc.sync.dma_start(out=w3_raw[:], in_=w3.rearrange("(p j) c -> p j c", j=PACK))
+
+        def reciprocals(pc):
+            n = pieces.index(pc)
+            pre_b = ring.tile([P, HALF], F32, name="pre_b")
+            pre_a = ring.tile([P, HALF], F32, name="pre_a")
+            if n < 2:
+                nc.vector.scalar_tensor_tensor(pre_b[:], rad_sb[pc][:], 1.0, rad_sb[pc][:], ALU.add, ALU.mult)
+                nc.scalar.activation(inv_b[pc][:], pre_b[:], ACT.Abs_reciprocal_sqrt, bias=0.25)
+            else:
+                nc.scalar.activation(pre_b[:], rad_sb[pc][:], ACT.Abs_reciprocal_sqrt, bias=0.5)
+            if n < 2:
+                nc.vector.tensor_tensor(pre_a[:], rad_sb[pc][:], rad_sb[pc][:], ALU.mult)
+                nc.scalar.activation(inv_a[pc][:], pre_a[:], ACT.Abs_reciprocal_sqrt)
+            else:
+                nc.scalar.activation(pre_a[:], rad_sb[pc][:], ACT.Abs_reciprocal_sqrt)
+                nc.scalar.activation(inv_a[pc][:], pre_a[:], ACT.Square)
+            if n >= 2:
+                nc.scalar.activation(inv_b[pc][:], pre_b[:], ACT.Square)
+
+        def quantize(grouped, name):
+            width = grouped.shape[1] // PACK
+            codes = keep.tile([P, width], U32, name=name + "_codes", align_bytes=64)
+            scales = keep.tile([P, width], U8, name=name + "_scales", align_bytes=64)
+            nc.vector.quantize_mx(out=codes[:].bitcast(FP8X4), scales=scales[:], in_=grouped[:])
+            return codes, scales
+
+        reciprocals(pieces[0])
+        xg_codes = keep.tile([P, S], U32, name="xg_codes", align_bytes=64)
+        xg_scales = keep.tile([P, S], U8, name="xg_scales", align_bytes=64)
+        nc.vector.tensor_copy(xg_codes[:], xw[:].bitcast(U32).indirect(offs_sb[:]))
+        nc.vector.tensor_copy(xg_scales[:], xs[:].indirect(offs_sb[:]))
+
+        unit_abs = keep.tile([P, PACK], F32, name="unit_abs")
+        scale_a = keep.tile([P, PACK], F32, name="scale_a")
+        scale_b = keep.tile([P, PACK], F32, name="scale_b")
+        floor = keep.tile([P, PACK], F32, name="floor")
+        unit_ge = keep.tile([P, PACK], F32, name="unit_ge")
+        unit_sign = keep.tile([P, PACK], F32, name="unit_sign")
+        nc.vector.scalar_tensor_tensor(unit_abs[:], unit_sb[:], -1.0, unit_sb[:], ALU.mult, ALU.max)
+        nc.vector.tensor_scalar(unit_ge[:], unit_sb[:], 0.0, 2.0, ALU.is_ge, ALU.mult)
+        nc.vector.scalar_tensor_tensor(floor[:], unit_sb[:], 0.05, unit_sb[:], ALU.mult, ALU.mult)
+        nc.vector.tensor_scalar_mul(scale_a[:], unit_abs[:], 0.5)
+        nc.vector.tensor_scalar_mul(scale_b[:], unit_abs[:], 1.25)
+        nc.vector.tensor_scalar_add(unit_sign[:], unit_ge[:], -1.0)
+
+        def first_product(w_raw, scale, name, on_scalar):
+            grouped = keep.tile([P, PACK * H], BF16, name=name + "_grouped", align_bytes=64)
+            dealt = grouped[:].rearrange("p (t m j) -> p m j t", t=PACK, j=PACK)
+            rows = w_raw[:].rearrange("p j (m t) -> p m j t", t=PACK)
+            nc.vector.tensor_copy(out=dealt[:, on_scalar:], in_=rows[:, on_scalar:])
+            if on_scalar:
+                nc.scalar.copy(dealt[:, :on_scalar], rows[:, :on_scalar])
+            codes, scales = quantize(grouped, name)
+            windows = []
+            for t in range(PACK):
+                acc = psum.tile([P, S], F32, name="acc")
+                cols = slice(t * P, (t + 1) * P)
+                nc.tensor.matmul_mx(out=acc[:], lhsT=codes[:, cols].bitcast(FP8X4), lhsT_scale=scales[:, cols],
+                                    rhs=xg_codes[:].bitcast(FP8X4), rhs_scale=xg_scales[:], start=True, stop=True)
+                window = keep.tile([P, S], F32, name="%s_window_%d" % (name, t))
+                nc.scalar.activation(window[:], acc[:], ACT.Copy, scale=scale[:, t : t + 1])
+                windows.append(window)
+            return windows
+
+        for pc in pieces[1:1]:
+            reciprocals(pc)
+        win_a = first_product(w1_raw, scale_a, "w1", 48)
+        for pc in pieces[1:4]:
+            reciprocals(pc)
+        win_b = first_product(w2_raw, scale_b, "w2", 0)
+        for pc in pieces[4:6]:
+            reciprocals(pc)
+
+        groups = U // GROUP
+        part_a = [keep.tile([P, PACK * GROUP], F32, name="part_a_%d" % g) for g in range(groups)]
+        part_b = [keep.tile([P, PACK * GROUP], F32, name="part_b_%d" % g) for g in range(groups)]
+        alone_sq = [keep.tile([P, PACK * GROUP], F32, name="alone_sq_%d" % g) for g in range(groups)]
+        mixed_sq = [keep.tile([P, PACK * GROUP], F32, name="mixed_sq_%d" % g) for g in range(groups)]
+        blocks = 2 * GROUP // P
+        steps = [(g, pair) for g in range(groups) for pair in range(2)]
+        on_vector = steps[len(steps) - 3 :]
+
+        def squares(g, pair):
+            half, r0 = divmod(g * GROUP, HALF)
+            cols = slice(r0, r0 + GROUP)
+            entries = slice(g * GROUP // LIST_COL, (g + 1) * GROUP // LIST_COL)
+            for j in (2 * pair, 2 * pair + 1):
+                nc.vector.tensor_tensor(part_a[g][:, j * GROUP : (j + 1) * GROUP], win_a[j][:].indirect(pa_sb[:, entries]), inv_a[(half, j)][:, cols], ALU.mult)
+            for j in (2 * pair, 2 * pair + 1):
+                nc.vector.tensor_tensor(part_b[g][:, j * GROUP : (j + 1) * GROUP], win_b[j][:].indirect(pb_sb[:, entries]), inv_b[(half, j)][:, cols], ALU.mult)
+            base = pair * 2 * GROUP
+            if (g, pair) in on_vector:
+                both = slice(base, base + 2 * GROUP)
+                nc.scalar.activation(alone_sq[g][:, both], part_a[g][:, both], ACT.Square, scale=2.0 * math.sqrt(0.84))
+                mixed_sb = ring.tile([P, 2 * GROUP], F32, name="mixed_sb")
+                nc.vector.tensor_tensor(mixed_sb[:], part_a[g][:, both], part_b[g][:, both], ALU.add)
+                nc.scalar.activation(mixed_sq[g][:, both], mixed_sb[:], ACT.Square, scale=0.8)
+                return
+            alone = psum.tile([P, 2 * GROUP], F32, name="alone")
+            mixed = psum.tile([P, 2 * GROUP], F32, name="mixed")
+            for b in range(blocks):
+                nc.tensor.transpose(alone[:, b * P : (b + 1) * P], part_a[g][:, base + b * P : base + (b + 1) * P], ident[:])
+            for b in range(blocks):
+                blk = slice(b * P, (b + 1) * P)
+                src = slice(base + b * P, base + (b + 1) * P)
+                nc.tensor.matmul(mixed[:, blk], lhsT=part_a[g][:, src], rhs=ident[:], is_transpose=True, start=True, stop=False)
+                nc.tensor.matmul(mixed[:, blk], lhsT=part_b[g][:, src], rhs=ident[:], is_transpose=True, start=False, stop=True)
+            nc.scalar.activation(alone_sq[g][:, base : base + 2 * GROUP], alone[:], ACT.Square, scale=2.0 * math.sqrt(0.84))
+            nc.scalar.activation(mixed_sq[g][:, base : base + 2 * GROUP], mixed[:], ACT.Square, scale=0.8)
+
+        amp = {}
+
+        def amplitude(g, pair):
+            base = pair * 2 * GROUP
+            if (g, pair) in on_vector:
+                form = ring.tile([P, 2 * GROUP], F32, name="form_sb")
+                nc.vector.tensor_tensor(form[:], alone_sq[g][:, base : base + 2 * GROUP], mixed_sq[g][:, base : base + 2 * GROUP], ALU.add)
+            else:
+                form = psum.tile([P, 2 * GROUP], F32, name="form")
+                for b in range(blocks):
+                    blk = slice(b * P, (b + 1) * P)
+                    src = slice(base + b * P, base + (b + 1) * P)
+                    nc.tensor.matmul(form[:, blk], lhsT=alone_sq[g][:, src], rhs=ident[:], is_transpose=True, start=True, stop=False)
+                    nc.tensor.matmul(form[:, blk], lhsT=mixed_sq[g][:, src], rhs=ident[:], is_transpose=True, start=False, stop=True)
+            if pair == 0:
+                amp[g] = keep.tile([P, PACK * GROUP], F32, name="amp_%d" % g, tag="rad_%d_%d" % pieces[-1 - g])
+            for jj in range(2):
+                j = 2 * pair + jj
+                nc.scalar.activation(amp[g][:, j * GROUP : (j + 1) * GROUP], form[:, jj * GROUP : (jj + 1) * GROUP], ACT.Sqrt, bias=floor[:, j : j + 1])
+
+        def finish(g):
+            hid = ring.tile([P, PACK * GROUP], BF16, name="hid", align_bytes=64)
+            nc.vector.tensor_tensor(
+                hid[:].rearrange("p (c i j) -> p c j i", i=4, j=PACK),
+                amp[g][:].rearrange("p (j c i) -> p c j i", i=4, j=PACK),
+                part_a[g][:].rearrange("p (j c i) -> p c j i", i=4, j=PACK),
+                ALU.subtract,
+            )
+            hid_codes, hid_scales = quantize(hid, "hid_%d" % g)
+            acc = psum.tile([P, N // P * GROUP], F32, name="acc")
+            for mt in range(N // P):
+                mcols = slice(mt * P, (mt + 1) * P)
+                nc.tensor.matmul_mx(out=acc[:, mt * GROUP : (mt + 1) * GROUP], lhsT=w3_codes[:, mcols].bitcast(FP8X4), lhsT_scale=w3_scales[:, mcols],
+                                    rhs=hid_codes[:].bitcast(FP8X4), rhs_scale=hid_scales[:], start=True, stop=True)
+            result = ring.tile([P, N // P, GROUP], F32, name="result")
+            nc.vector.tensor_copy(result[:].rearrange("p mt r -> p (mt r)"), acc[:])
+            nc.sync.dma_start(out=out_rows[:, :, g * GROUP : (g + 1) * GROUP], in_=result[:])
+
+        w3_grouped = keep.tile([P, PACK * N], BF16, name="w3_grouped", align_bytes=64)
+        nc.vector.tensor_tensor(
+            w3_grouped[:].rearrange("p (c i j) -> p c j i", i=4, j=PACK),
+            w3_raw[:].rearrange("p j (c i) -> p c j i", i=4),
+            unit_sign[:].unsqueeze(1).unsqueeze(3).to_broadcast([P, N // 4, PACK, 4]),
+            ALU.mult,
+        )
+        w3_codes, w3_scales = quantize(w3_grouped, "w3")
+        out_rows = out.rearrange("(mt p) r -> p mt r", p=P)
+
+        for step, pc in zip(steps, pieces[6:]):
+            squares(*step)
+            reciprocals(pc)
+        for step in steps[2:2]:
+            squares(*step)
+        for i, step in enumerate(steps):
+            if i + 2 < len(steps):
+                squares(*steps[i + 2])
+            amplitude(*step)
+            if i % 2 == 1:
+                finish(i // 2)

@@ -20,7 +20,9 @@ ACT = mybir.ActivationFunctionType
 P = 128
 PACK = 4
 HALF = 512
-GROUP = 256
+WIDTHS = (512, 256, 128, 128)
+STEP = 256
+SPARE = 8
 LIST_COL = 16
 
 
@@ -55,40 +57,40 @@ def tile_picked_yacoust_amp_p_kernel(tc, x_words, x_scales, w1, w2, rad, unit, w
 
         load_rad(pieces[0])
         load_rad(pieces[1])
+        load_rad(pieces[2])
+        load_rad(pieces[3])
         nc.sync.dma_start(out=w1_raw[:], in_=w1.rearrange("(p j) c -> p j c", j=PACK))
         nc.sync.dma_start(offs_sb[:], offs)
         for q in range(4):
             nc.sync.dma_start(out=xs[32 * q : 32 * q + 4, :].bitcast(I32), in_=x_scales[0, 4 * q : 4 * q + 4, :].bitcast(I32))
         make_identity(nc, ident[:])
-        load_rad(pieces[2])
         nc.sync.dma_start(out=xw[:], in_=x_words[0].rearrange("p n t -> p (n t)").bitcast(I32))
         nc.sync.dma_start(out=unit_sb[:], in_=unit.rearrange("(p j) o -> p (j o)", j=PACK))
         nc.sync.dma_start(pa_sb[:], pa)
         nc.sync.dma_start(pb_sb[:], pb)
         nc.sync.dma_start(out=w2_raw[:], in_=w2.rearrange("(p j) c -> p j c", j=PACK))
-        load_rad(pieces[3])
         load_rad(pieces[4])
+        nc.sync.dma_start(out=w3_raw[:], in_=w3.rearrange("(p j) c -> p j c", j=PACK))
         load_rad(pieces[5])
         load_rad(pieces[6])
         load_rad(pieces[7])
-        nc.sync.dma_start(out=w3_raw[:], in_=w3.rearrange("(p j) c -> p j c", j=PACK))
 
         def reciprocals(pc):
             n = pieces.index(pc)
             pre_b = ring.tile([P, HALF], F32, name="pre_b")
             pre_a = ring.tile([P, HALF], F32, name="pre_a")
-            if n < 2:
+            if n < 0:
                 nc.vector.scalar_tensor_tensor(pre_b[:], rad_sb[pc][:], 1.0, rad_sb[pc][:], ALU.add, ALU.mult)
                 nc.scalar.activation(inv_b[pc][:], pre_b[:], ACT.Abs_reciprocal_sqrt, bias=0.25)
             else:
                 nc.scalar.activation(pre_b[:], rad_sb[pc][:], ACT.Abs_reciprocal_sqrt, bias=0.5)
-            if n < 2:
+            if n < 5:
                 nc.vector.tensor_tensor(pre_a[:], rad_sb[pc][:], rad_sb[pc][:], ALU.mult)
                 nc.scalar.activation(inv_a[pc][:], pre_a[:], ACT.Abs_reciprocal_sqrt)
             else:
                 nc.scalar.activation(pre_a[:], rad_sb[pc][:], ACT.Abs_reciprocal_sqrt)
                 nc.scalar.activation(inv_a[pc][:], pre_a[:], ACT.Square)
-            if n >= 2:
+            if n >= 0:
                 nc.scalar.activation(inv_b[pc][:], pre_b[:], ACT.Square)
 
         def quantize(grouped, name):
@@ -127,83 +129,87 @@ def tile_picked_yacoust_amp_p_kernel(tc, x_words, x_scales, w1, w2, rad, unit, w
             codes, scales = quantize(grouped, name)
             windows = []
             for t in range(PACK):
-                acc = psum.tile([P, S], F32, name="acc")
+                acc = psum.tile([P, S], F32, name="acc", bufs=2)
                 cols = slice(t * P, (t + 1) * P)
                 nc.tensor.matmul_mx(out=acc[:], lhsT=codes[:, cols].bitcast(FP8X4), lhsT_scale=scales[:, cols],
                                     rhs=xg_codes[:].bitcast(FP8X4), rhs_scale=xg_scales[:], start=True, stop=True)
-                window = keep.tile([P, S], F32, name="%s_window_%d" % (name, t))
-                nc.scalar.activation(window[:], acc[:], ACT.Copy, scale=scale[:, t : t + 1])
+                window = keep.tile([P, S + SPARE], F32, name="%s_window_%d" % (name, t))
+                nc.gpsimd.memset(window[:, S:], 0.0)
+                nc.scalar.activation(window[:, :S], acc[:], ACT.Copy, scale=scale[:, t : t + 1])
                 windows.append(window)
             return windows
 
         for pc in pieces[1:1]:
             reciprocals(pc)
-        win_a = first_product(w1_raw, scale_a, "w1", 48)
+        win_a = first_product(w1_raw, scale_a, "w1", 32)
         for pc in pieces[1:4]:
             reciprocals(pc)
         win_b = first_product(w2_raw, scale_b, "w2", 0)
         for pc in pieces[4:6]:
             reciprocals(pc)
 
-        groups = U // GROUP
-        part_a = [keep.tile([P, PACK * GROUP], F32, name="part_a_%d" % g) for g in range(groups)]
-        part_b = [keep.tile([P, PACK * GROUP], F32, name="part_b_%d" % g) for g in range(groups)]
-        alone_sq = [keep.tile([P, PACK * GROUP], F32, name="alone_sq_%d" % g) for g in range(groups)]
-        mixed_sq = [keep.tile([P, PACK * GROUP], F32, name="mixed_sq_%d" % g) for g in range(groups)]
-        blocks = 2 * GROUP // P
-        steps = [(g, pair) for g in range(groups) for pair in range(2)]
-        on_vector = steps[len(steps) - 3 :]
+        groups = range(len(WIDTHS))
+        first = [sum(WIDTHS[:g]) for g in groups]
+        part_a = [keep.tile([P, PACK * WIDTHS[g]], F32, name="part_a_%d" % g) for g in groups]
+        part_b = [keep.tile([P, PACK * WIDTHS[g]], F32, name="part_b_%d" % g) for g in groups]
+        alone_sq = [keep.tile([P, PACK * WIDTHS[g]], F32, name="alone_sq_%d" % g) for g in groups]
+        mixed_sq = [keep.tile([P, PACK * WIDTHS[g]], F32, name="mixed_sq_%d" % g) for g in groups]
+        steps = []
+        for g in groups:
+            count = max(1, min(PACK, STEP // WIDTHS[g]))
+            steps.extend((g, range(j, j + count)) for j in range(0, PACK, count))
+        on_vector = steps[len(steps) - 4 :]
 
-        def squares(g, pair):
-            half, r0 = divmod(g * GROUP, HALF)
-            cols = slice(r0, r0 + GROUP)
-            entries = slice(g * GROUP // LIST_COL, (g + 1) * GROUP // LIST_COL)
-            for j in (2 * pair, 2 * pair + 1):
-                nc.vector.tensor_tensor(part_a[g][:, j * GROUP : (j + 1) * GROUP], win_a[j][:].indirect(pa_sb[:, entries]), inv_a[(half, j)][:, cols], ALU.mult)
-            for j in (2 * pair, 2 * pair + 1):
-                nc.vector.tensor_tensor(part_b[g][:, j * GROUP : (j + 1) * GROUP], win_b[j][:].indirect(pb_sb[:, entries]), inv_b[(half, j)][:, cols], ALU.mult)
-            base = pair * 2 * GROUP
-            if (g, pair) in on_vector:
-                both = slice(base, base + 2 * GROUP)
-                nc.scalar.activation(alone_sq[g][:, both], part_a[g][:, both], ACT.Square, scale=2.0 * math.sqrt(0.84))
-                mixed_sb = ring.tile([P, 2 * GROUP], F32, name="mixed_sb")
-                nc.vector.tensor_tensor(mixed_sb[:], part_a[g][:, both], part_b[g][:, both], ALU.add)
-                nc.scalar.activation(mixed_sq[g][:, both], mixed_sb[:], ACT.Square, scale=0.8)
-                return
-            alone = psum.tile([P, 2 * GROUP], F32, name="alone")
-            mixed = psum.tile([P, 2 * GROUP], F32, name="mixed")
-            for b in range(blocks):
-                nc.tensor.transpose(alone[:, b * P : (b + 1) * P], part_a[g][:, base + b * P : base + (b + 1) * P], ident[:])
-            for b in range(blocks):
-                blk = slice(b * P, (b + 1) * P)
-                src = slice(base + b * P, base + (b + 1) * P)
-                nc.tensor.matmul(mixed[:, blk], lhsT=part_a[g][:, src], rhs=ident[:], is_transpose=True, start=True, stop=False)
-                nc.tensor.matmul(mixed[:, blk], lhsT=part_b[g][:, src], rhs=ident[:], is_transpose=True, start=False, stop=True)
-            nc.scalar.activation(alone_sq[g][:, base : base + 2 * GROUP], alone[:], ACT.Square, scale=2.0 * math.sqrt(0.84))
-            nc.scalar.activation(mixed_sq[g][:, base : base + 2 * GROUP], mixed[:], ACT.Square, scale=0.8)
+        def add_turned(bank, span, *terms):
+            for b in range((span.stop - span.start) // P):
+                src = slice(span.start + b * P, span.start + (b + 1) * P)
+                for n, term in enumerate(terms):
+                    nc.tensor.matmul(bank[:, b * P : (b + 1) * P], lhsT=term[:, src], rhs=ident[:], is_transpose=True, start=(n == 0), stop=(n == len(terms) - 1))
+
+        def squares(g, planes):
+            width = WIDTHS[g]
+            half, r0 = divmod(first[g], HALF)
+            cols = slice(r0, r0 + width)
+            entries = slice(first[g] // LIST_COL, (first[g] + width) // LIST_COL)
+            for j in planes:
+                nc.vector.tensor_tensor(part_a[g][:, j * width : (j + 1) * width], win_a[j][:].indirect(pa_sb[:, entries]), inv_a[(half, j)][:, cols], ALU.mult)
+            for j in planes:
+                nc.vector.tensor_tensor(part_b[g][:, j * width : (j + 1) * width], win_b[j][:].indirect(pb_sb[:, entries]), inv_b[(half, j)][:, cols], ALU.mult)
+            span = slice(planes.start * width, planes.stop * width)
+            n = span.stop - span.start
+            if (g, planes) in on_vector:
+                nc.scalar.activation(alone_sq[g][:, span], part_a[g][:, span], ACT.Square, scale=2.0 * math.sqrt(0.84))
+                mixed = ring.tile([P, n], F32, name="mixed_sb")
+                nc.vector.tensor_tensor(mixed[:], part_a[g][:, span], part_b[g][:, span], ALU.add)
+            else:
+                alone = psum.tile([P, n], F32, name="alone", bufs=2)
+                mixed = psum.tile([P, n], F32, name="mixed", bufs=2)
+                add_turned(alone, span, part_a[g])
+                add_turned(mixed, span, part_a[g], part_b[g])
+                nc.scalar.activation(alone_sq[g][:, span], alone[:], ACT.Square, scale=2.0 * math.sqrt(0.84))
+            nc.scalar.activation(mixed_sq[g][:, span], mixed[:], ACT.Square, scale=0.8)
 
         amp = {}
 
-        def amplitude(g, pair):
-            base = pair * 2 * GROUP
-            if (g, pair) in on_vector:
-                form = ring.tile([P, 2 * GROUP], F32, name="form_sb")
-                nc.vector.tensor_tensor(form[:], alone_sq[g][:, base : base + 2 * GROUP], mixed_sq[g][:, base : base + 2 * GROUP], ALU.add)
+        def amplitude(g, planes):
+            width = WIDTHS[g]
+            span = slice(planes.start * width, planes.stop * width)
+            n = span.stop - span.start
+            if (g, planes) in on_vector:
+                form = ring.tile([P, n], F32, name="form_sb")
+                nc.vector.tensor_tensor(form[:], alone_sq[g][:, span], mixed_sq[g][:, span], ALU.add)
             else:
-                form = psum.tile([P, 2 * GROUP], F32, name="form")
-                for b in range(blocks):
-                    blk = slice(b * P, (b + 1) * P)
-                    src = slice(base + b * P, base + (b + 1) * P)
-                    nc.tensor.matmul(form[:, blk], lhsT=alone_sq[g][:, src], rhs=ident[:], is_transpose=True, start=True, stop=False)
-                    nc.tensor.matmul(form[:, blk], lhsT=mixed_sq[g][:, src], rhs=ident[:], is_transpose=True, start=False, stop=True)
-            if pair == 0:
-                amp[g] = keep.tile([P, PACK * GROUP], F32, name="amp_%d" % g, tag="rad_%d_%d" % pieces[-1 - g])
-            for jj in range(2):
-                j = 2 * pair + jj
-                nc.scalar.activation(amp[g][:, j * GROUP : (j + 1) * GROUP], form[:, jj * GROUP : (jj + 1) * GROUP], ACT.Sqrt, bias=floor[:, j : j + 1])
+                form = psum.tile([P, n], F32, name="form", bufs=2)
+                add_turned(form, span, alone_sq[g], mixed_sq[g])
+            if planes.start == 0:
+                amp[g] = keep.tile([P, PACK * width], F32, name="amp_%d" % g, tag="rad_%d_%d" % pieces[-1 - g])
+            for j in planes:
+                at = (j - planes.start) * width
+                nc.scalar.activation(amp[g][:, j * width : (j + 1) * width], form[:, at : at + width], ACT.Sqrt, bias=floor[:, j : j + 1])
 
         def finish(g):
-            hid = ring.tile([P, PACK * GROUP], BF16, name="hid", align_bytes=64)
+            width = WIDTHS[g]
+            hid = ring.tile([P, PACK * width], BF16, name="hid", align_bytes=64)
             nc.vector.tensor_tensor(
                 hid[:].rearrange("p (c i j) -> p c j i", i=4, j=PACK),
                 amp[g][:].rearrange("p (j c i) -> p c j i", i=4, j=PACK),
@@ -211,14 +217,19 @@ def tile_picked_yacoust_amp_p_kernel(tc, x_words, x_scales, w1, w2, rad, unit, w
                 ALU.subtract,
             )
             hid_codes, hid_scales = quantize(hid, "hid_%d" % g)
-            acc = psum.tile([P, N // P * GROUP], F32, name="acc")
-            for mt in range(N // P):
-                mcols = slice(mt * P, (mt + 1) * P)
-                nc.tensor.matmul_mx(out=acc[:, mt * GROUP : (mt + 1) * GROUP], lhsT=w3_codes[:, mcols].bitcast(FP8X4), lhsT_scale=w3_scales[:, mcols],
-                                    rhs=hid_codes[:].bitcast(FP8X4), rhs_scale=hid_scales[:], start=True, stop=True)
-            result = ring.tile([P, N // P, GROUP], F32, name="result")
-            nc.vector.tensor_copy(result[:].rearrange("p mt r -> p (mt r)"), acc[:])
-            nc.sync.dma_start(out=out_rows[:, :, g * GROUP : (g + 1) * GROUP], in_=result[:])
+            n = min(width, HALF * P // N)
+            for r0 in range(0, width, n):
+                acc = psum.tile([P, N // P * n], F32, name="acc", bufs=2)
+                for mt in range(N // P):
+                    mcols = slice(mt * P, (mt + 1) * P)
+                    nc.tensor.matmul_mx(out=acc[:, mt * n : (mt + 1) * n], lhsT=w3_codes[:, mcols].bitcast(FP8X4), lhsT_scale=w3_scales[:, mcols],
+                                        rhs=hid_codes[:, r0 : r0 + n].bitcast(FP8X4), rhs_scale=hid_scales[:, r0 : r0 + n], start=True, stop=True)
+                result = ring.tile([P, N // P, n], F32, name="result")
+                if "SSSV"[min(g, 3)] == "S":
+                    nc.scalar.copy(result[:].rearrange("p mt r -> p (mt r)"), acc[:])
+                else:
+                    nc.vector.tensor_copy(result[:].rearrange("p mt r -> p (mt r)"), acc[:])
+                nc.sync.dma_start(out=out_rows[:, :, first[g] + r0 : first[g] + r0 + n], in_=result[:])
 
         w3_grouped = keep.tile([P, PACK * N], BF16, name="w3_grouped", align_bytes=64)
         nc.vector.tensor_tensor(
@@ -239,5 +250,5 @@ def tile_picked_yacoust_amp_p_kernel(tc, x_words, x_scales, w1, w2, rad, unit, w
             if i + 2 < len(steps):
                 squares(*steps[i + 2])
             amplitude(*step)
-            if i % 2 == 1:
-                finish(i // 2)
+            if step[1].stop == PACK:
+                finish(step[0])

@@ -58,20 +58,20 @@ def tile_picked_yacoust_amp_p_kernel(tc, x_words, x_scales, w1, w2, rad, unit, w
         load_rad(pieces[0])
         load_rad(pieces[1])
         load_rad(pieces[2])
-        load_rad(pieces[3])
         nc.sync.dma_start(out=w1_raw[:], in_=w1.rearrange("(p j) c -> p j c", j=PACK))
         nc.sync.dma_start(offs_sb[:], offs)
+        nc.sync.dma_start(out=unit_sb[:], in_=unit.rearrange("(p j) o -> p (j o)", j=PACK))
         for q in range(4):
             nc.sync.dma_start(out=xs[32 * q : 32 * q + 4, :].bitcast(I32), in_=x_scales[0, 4 * q : 4 * q + 4, :].bitcast(I32))
         make_identity(nc, ident[:])
         nc.sync.dma_start(out=xw[:], in_=x_words[0].rearrange("p n t -> p (n t)").bitcast(I32))
-        nc.sync.dma_start(out=unit_sb[:], in_=unit.rearrange("(p j) o -> p (j o)", j=PACK))
-        nc.sync.dma_start(pa_sb[:], pa)
-        nc.sync.dma_start(pb_sb[:], pb)
+        load_rad(pieces[3])
         nc.sync.dma_start(out=w2_raw[:], in_=w2.rearrange("(p j) c -> p j c", j=PACK))
+        nc.sync.dma_start(pa_sb[:], pa)
         load_rad(pieces[4])
-        nc.sync.dma_start(out=w3_raw[:], in_=w3.rearrange("(p j) c -> p j c", j=PACK))
+        nc.sync.dma_start(pb_sb[:], pb)
         load_rad(pieces[5])
+        nc.sync.dma_start(out=w3_raw[:], in_=w3.rearrange("(p j) c -> p j c", j=PACK))
         load_rad(pieces[6])
         load_rad(pieces[7])
 
@@ -84,7 +84,7 @@ def tile_picked_yacoust_amp_p_kernel(tc, x_words, x_scales, w1, w2, rad, unit, w
                 nc.scalar.activation(inv_b[pc][:], pre_b[:], ACT.Abs_reciprocal_sqrt, bias=0.25)
             else:
                 nc.scalar.activation(pre_b[:], rad_sb[pc][:], ACT.Abs_reciprocal_sqrt, bias=0.5)
-            if n < 5:
+            if n < 3:
                 nc.vector.tensor_tensor(pre_a[:], rad_sb[pc][:], rad_sb[pc][:], ALU.mult)
                 nc.scalar.activation(inv_a[pc][:], pre_a[:], ACT.Abs_reciprocal_sqrt)
             else:
@@ -141,7 +141,7 @@ def tile_picked_yacoust_amp_p_kernel(tc, x_words, x_scales, w1, w2, rad, unit, w
 
         for pc in pieces[1:1]:
             reciprocals(pc)
-        win_a = first_product(w1_raw, scale_a, "w1", 32)
+        win_a = first_product(w1_raw, scale_a, "w1", 64)
         for pc in pieces[1:4]:
             reciprocals(pc)
         win_b = first_product(w2_raw, scale_b, "w2", 0)
@@ -225,12 +225,17 @@ def tile_picked_yacoust_amp_p_kernel(tc, x_words, x_scales, w1, w2, rad, unit, w
                     nc.tensor.matmul_mx(out=acc[:, mt * n : (mt + 1) * n], lhsT=w3_codes[:, mcols].bitcast(FP8X4), lhsT_scale=w3_scales[:, mcols],
                                         rhs=hid_codes[:, r0 : r0 + n].bitcast(FP8X4), rhs_scale=hid_scales[:, r0 : r0 + n], start=True, stop=True)
                 result = ring.tile([P, N // P, n], F32, name="result")
-                if "SSSV"[min(g, 3)] == "S":
+                if "S"[min(g, 0)] == "S":
                     nc.scalar.copy(result[:].rearrange("p mt r -> p (mt r)"), acc[:])
                 else:
                     nc.vector.tensor_copy(result[:].rearrange("p mt r -> p (mt r)"), acc[:])
                 nc.sync.dma_start(out=out_rows[:, :, first[g] + r0 : first[g] + r0 + n], in_=result[:])
 
+        for step, pc in zip(steps, pieces[6:]):
+            squares(*step)
+            reciprocals(pc)
+        for step in steps[2:2]:
+            squares(*step)
         w3_grouped = keep.tile([P, PACK * N], BF16, name="w3_grouped", align_bytes=64)
         nc.vector.tensor_tensor(
             w3_grouped[:].rearrange("p (c i j) -> p c j i", i=4, j=PACK),
@@ -241,11 +246,6 @@ def tile_picked_yacoust_amp_p_kernel(tc, x_words, x_scales, w1, w2, rad, unit, w
         w3_codes, w3_scales = quantize(w3_grouped, "w3")
         out_rows = out.rearrange("(mt p) r -> p mt r", p=P)
 
-        for step, pc in zip(steps, pieces[6:]):
-            squares(*step)
-            reciprocals(pc)
-        for step in steps[2:2]:
-            squares(*step)
         for i, step in enumerate(steps):
             if i + 2 < len(steps):
                 squares(*steps[i + 2])

import math
from contextlib import ExitStack

import concourse.mybir as mybir
from concourse.masks import make_identity

K, T, S, N, H, U = 512, 2048, 512, 256, 512, 1024
FLOPS = 2 * K * H * S * 2 + 2 * H * N * U

F32 = mybir.dt.float32
BF16 = mybir.dt.bfloat16
I32 = mybir.dt.int32
U32 = mybir.dt.uint32
U16 = mybir.dt.uint16
U8 = mybir.dt.uint8
FP8X4 = mybir.dt.float8_e4m3fn_x4
ALU = mybir.AluOpType
ACT = mybir.ActivationFunctionType

P = 128
PACK = 4
HALF = 512
WIDTHS = (512, 256, 128, 128)
STEP = 256
SPARE = 8
LIST_COL = 16


def tile_picked_yacoust_amp_p_kernel(tc, x_words, x_scales, w1, w2, rad, unit, w3, offs, pa, pb, out):
    nc = tc.nc
    with ExitStack() as ctx:
        keep = ctx.enter_context(tc.tile_pool(name="keep", bufs=1))
        ring = ctx.enter_context(tc.tile_pool(name="ring", bufs=3))
        psum = ctx.enter_context(tc.psum_pool(name="psum", bufs=2))

        offs_sb = keep.tile([P, S // LIST_COL], U16, name="offs_sb")
        pa_sb = keep.tile([P, U // LIST_COL], U16, name="pa_sb")
        pb_sb = keep.tile([P, U // LIST_COL], U16, name="pb_sb")
        xw = keep.tile([P, T], I32, name="xw")
        xs = keep.tile([P, T], U8, name="xs")
        w1_raw = keep.tile([P, PACK, H], F32, name="w1_raw")
        w2_raw = keep.tile([P, PACK, H], F32, name="w2_raw")
        w3_raw = keep.tile([P, PACK, N], F32, name="w3_raw")
        unit_sb = keep.tile([P, PACK], F32, name="unit_sb")
        ident = keep.tile([P, P], F32, name="ident")
        pieces = [(half, j) for half in range(U // HALF) for j in range(PACK)]
        rad_sb = {pc: keep.tile([P, HALF], F32, name="rad_%d_%d" % pc, tag="rad_%d_%d" % pc) for pc in pieces}
        inv_a = {pc: keep.tile([P, HALF], F32, name="inv_a_%d_%d" % pc) for pc in pieces}
        inv_b = {pc: keep.tile([P, HALF], F32, name="inv_b_%d_%d" % pc) for pc in pieces}
        rad_rows = rad.rearrange("(p j) r -> p j r", j=PACK)

        def load_rad(pc):
            half, j = pc
            nc.sync.dma_start(out=rad_sb[pc][:], in_=rad_rows[:, j, half * HALF : (half + 1) * HALF])

        nc.vector.memset(xs[:].bitcast(I32), 0)

        load_rad(pieces[0])
        load_rad(pieces[1])
        load_rad(pieces[2])
        nc.sync.dma_start(out=w1_raw[:], in_=w1.rearrange("(p j) c -> p j c", j=PACK))
        nc.sync.dma_start(offs_sb[:], offs)
        nc.sync.dma_start(out=unit_sb[:], in_=unit.rearrange("(p j) o -> p (j o)", j=PACK))
        for q in range(4):
            nc.sync.dma_start(out=xs[32 * q : 32 * q + 4, :].bitcast(I32), in_=x_scales[0, 4 * q : 4 * q + 4, :].bitcast(I32))
        make_identity(nc, ident[:])
        nc.sync.dma_start(out=xw[:], in_=x_words[0].rearrange("p n t -> p (n t)").bitcast(I32))
        load_rad(pieces[3])
        nc.sync.dma_start(out=w2_raw[:], in_=w2.rearrange("(p j) c -> p j c", j=PACK))
        nc.sync.dma_start(pa_sb[:], pa)
        load_rad(pieces[4])
        nc.sync.dma_start(pb_sb[:], pb)
        load_rad(pieces[5])
        nc.sync.dma_start(out=w3_raw[:], in_=w3.rearrange("(p j) c -> p j c", j=PACK))
        load_rad(pieces[6])
        load_rad(pieces[7])

        def reciprocals(pc):
            n = pieces.index(pc)
            pre_b = ring.tile([P, HALF], F32, name="pre_b")
            pre_a = ring.tile([P, HALF], F32, name="pre_a")
            if n < 0:
                nc.vector.scalar_tensor_tensor(pre_b[:], rad_sb[pc][:], 1.0, rad_sb[pc][:], ALU.add, ALU.mult)
                nc.scalar.activation(inv_b[pc][:], pre_b[:], ACT.Abs_reciprocal_sqrt, bias=0.25)
            else:
                nc.scalar.activation(pre_b[:], rad_sb[pc][:], ACT.Abs_reciprocal_sqrt, bias=0.5)
            if n < 3:
                nc.vector.tensor_tensor(pre_a[:], rad_sb[pc][:], rad_sb[pc][:], ALU.mult)
                nc.scalar.activation(inv_a[pc][:], pre_a[:], ACT.Abs_reciprocal_sqrt)
            else:
                nc.scalar.activation(pre_a[:], rad_sb[pc][:], ACT.Abs_reciprocal_sqrt)
                nc.scalar.activation(inv_a[pc][:], pre_a[:], ACT.Square)
            if n >= 0:
                nc.scalar.activation(inv_b[pc][:], pre_b[:], ACT.Square)

        def quantize(grouped, name):
            width = grouped.shape[1] // PACK
            codes = keep.tile([P, width], U32, name=name + "_codes", align_bytes=64)
            scales = keep.tile([P, width], U8, name=name + "_scales", align_bytes=64)
            nc.vector.quantize_mx(out=codes[:].bitcast(FP8X4), scales=scales[:], in_=grouped[:])
            return codes, scales

        reciprocals(pieces[0])
        xg_codes = keep.tile([P, S], U32, name="xg_codes", align_bytes=64)
        xg_scales = keep.tile([P, S], U8, name="xg_scales", align_bytes=64)
        nc.vector.tensor_copy(xg_codes[:], xw[:].bitcast(U32).indirect(offs_sb[:]))
        nc.vector.tensor_copy(xg_scales[:], xs[:].indirect(offs_sb[:]))

        unit_abs = keep.tile([P, PACK], F32, name="unit_abs")
        scale_a = keep.tile([P, PACK], F32, name="scale_a")
        scale_b = keep.tile([P, PACK], F32, name="scale_b")
        floor = keep.tile([P, PACK], F32, name="floor")
        unit_ge = keep.tile([P, PACK], F32, name="unit_ge")
        unit_sign = keep.tile([P, PACK], F32, name="unit_sign")
        nc.vector.scalar_tensor_tensor(unit_abs[:], unit_sb[:], -1.0, unit_sb[:], ALU.mult, ALU.max)
        nc.vector.tensor_scalar(unit_ge[:], unit_sb[:], 0.0, 2.0, ALU.is_ge, ALU.mult)
        nc.vector.scalar_tensor_tensor(floor[:], unit_sb[:], 0.05, unit_sb[:], ALU.mult, ALU.mult)
        nc.vector.tensor_scalar_mul(scale_a[:], unit_abs[:], 0.5)
        nc.vector.tensor_scalar_mul(scale_b[:], unit_abs[:], 1.25)
        nc.vector.tensor_scalar_add(unit_sign[:], unit_ge[:], -1.0)

        def first_product(w_raw, scale, name, on_scalar):
            grouped = keep.tile([P, PACK * H], BF16, name=name + "_grouped", align_bytes=64)
            dealt = grouped[:].rearrange("p (t m j) -> p m j t", t=PACK, j=PACK)
            rows = w_raw[:].rearrange("p j (m t) -> p m j t", t=PACK)
            nc.vector.tensor_copy(out=dealt[:, on_scalar:], in_=rows[:, on_scalar:])
            if on_scalar:
                nc.scalar.copy(dealt[:, :on_scalar], rows[:, :on_scalar])
            codes, scales = quantize(grouped, name)
            windows = []
            for t in range(PACK):
                acc = psum.tile([P, S], F32, name="acc", bufs=2)
                cols = slice(t * P, (t + 1) * P)
                nc.tensor.matmul_mx(out=acc[:], lhsT=codes[:, cols].bitcast(FP8X4), lhsT_scale=scales[:, cols],
                                    rhs=xg_codes[:].bitcast(FP8X4), rhs_scale=xg_scales[:], start=True, stop=True)
                window = keep.tile([P, S + SPARE], F32, name="%s_window_%d" % (name, t))
                nc.gpsimd.memset(window[:, S:], 0.0)
                nc.scalar.activation(window[:, :S], acc[:], ACT.Copy, scale=scale[:, t : t + 1])
                windows.append(window)
            return windows

        for pc in pieces[1:1]:
            reciprocals(pc)
        win_a = first_product(w1_raw, scale_a, "w1", 64)
        for pc in pieces[1:4]:
            reciprocals(pc)
        win_b = first_product(w2_raw, scale_b, "w2", 0)
        for pc in pieces[4:6]:
            reciprocals(pc)

        groups = range(len(WIDTHS))
        first = [sum(WIDTHS[:g]) for g in groups]
        part_a = [keep.tile([P, PACK * WIDTHS[g]], F32, name="part_a_%d" % g) for g in groups]
        part_b = [keep.tile([P, PACK * WIDTHS[g]], F32, name="part_b_%d" % g) for g in groups]
        alone_sq = [keep.tile([P, PACK * WIDTHS[g]], F32, name="alone_sq_%d" % g) for g in groups]
        mixed_sq = [keep.tile([P, PACK * WIDTHS[g]], F32, name="mixed_sq_%d" % g) for g in groups]
        steps = []
        for g in groups:
            count = max(1, min(PACK, STEP // WIDTHS[g]))
            steps.extend((g, range(j, j + count)) for j in range(0, PACK, count))
        on_vector = steps[len(steps) - 4 :]

        def add_turned(bank, span, *terms):
            for b in range((span.stop - span.start) // P):
                src = slice(span.start + b * P, span.start + (b + 1) * P)
                for n, term in enumerate(terms):
                    nc.tensor.matmul(bank[:, b * P : (b + 1) * P], lhsT=term[:, src], rhs=ident[:], is_transpose=True, start=(n == 0), stop=(n == len(terms) - 1))

        def squares(g, planes):
            width = WIDTHS[g]
            half, r0 = divmod(first[g], HALF)
            cols = slice(r0, r0 + width)
            entries = slice(first[g] // LIST_COL, (first[g] + width) // LIST_COL)
            for j in planes:
                nc.vector.tensor_tensor(part_a[g][:, j * width : (j + 1) * width], win_a[j][:].indirect(pa_sb[:, entries]), inv_a[(half, j)][:, cols], ALU.mult)
            for j in planes:
                nc.vector.tensor_tensor(part_b[g][:, j * width : (j + 1) * width], win_b[j][:].indirect(pb_sb[:, entries]), inv_b[(half, j)][:, cols], ALU.mult)
            span = slice(planes.start * width, planes.stop * width)
            n = span.stop - span.start
            if (g, planes) in on_vector:
                nc.scalar.activation(alone_sq[g][:, span], part_a[g][:, span], ACT.Square, scale=2.0 * math.sqrt(0.84))
                mixed = ring.tile([P, n], F32, name="mixed_sb")
                nc.vector.tensor_tensor(mixed[:], part_a[g][:, span], part_b[g][:, span], ALU.add)
            else:
                alone = psum.tile([P, n], F32, name="alone", bufs=2)
                mixed = psum.tile([P, n], F32, name="mixed", bufs=2)
                add_turned(alone, span, part_a[g])
                add_turned(mixed, span, part_a[g], part_b[g])
                nc.scalar.activation(alone_sq[g][:, span], alone[:], ACT.Square, scale=2.0 * math.sqrt(0.84))
            nc.scalar.activation(mixed_sq[g][:, span], mixed[:], ACT.Square, scale=0.8)

        amp = {}

        def amplitude(g, planes):
            width = WIDTHS[g]
            span = slice(planes.start * width, planes.stop * width)
            n = span.stop - span.start
            if (g, planes) in on_vector:
                form = ring.tile([P, n], F32, name="form_sb")
                nc.vector.tensor_tensor(form[:], alone_sq[g][:, span], mixed_sq[g][:, span], ALU.add)
            else:
                form = psum.tile([P, n], F32, name="form", bufs=2)
                add_turned(form, span, alone_sq[g], mixed_sq[g])
            if planes.start == 0:
                amp[g] = keep.tile([P, PACK * width], F32, name="amp_%d" % g, tag="rad_%d_%d" % pieces[-1 - g])
            for j in planes:
                at = (j - planes.start) * width
                nc.scalar.activation(amp[g][:, j * width : (j + 1) * width], form[:, at : at + width], ACT.Sqrt, bias=floor[:, j : j + 1])

        def finish(g):
            width = WIDTHS[g]
            hid = ring.tile([P, PACK * width], BF16, name="hid", align_bytes=64)
            nc.vector.tensor_tensor(
                hid[:].rearrange("p (c i j) -> p c j i", i=4, j=PACK),
                amp[g][:].rearrange("p (j c i) -> p c j i", i=4, j=PACK),
                part_a[g][:].rearrange("p (j c i) -> p c j i", i=4, j=PACK),
                ALU.subtract,
            )
            hid_codes, hid_scales = quantize(hid, "hid_%d" % g)
            n = min(width, HALF * P // N)
            for r0 in range(0, width, n):
                acc = psum.tile([P, N // P * n], F32, name="acc", bufs=2)
                for mt in range(N // P):
                    mcols = slice(mt * P, (mt + 1) * P)
                    nc.tensor.matmul_mx(out=acc[:, mt * n : (mt + 1) * n], lhsT=w3_codes[:, mcols].bitcast(FP8X4), lhsT_scale=w3_scales[:, mcols],
                                        rhs=hid_codes[:, r0 : r0 + n].bitcast(FP8X4), rhs_scale=hid_scales[:, r0 : r0 + n], start=True, stop=True)
                result = ring.tile([P, N // P, n], F32, name="result")
                if "S"[min(g, 0)] == "S":
                    nc.scalar.copy(result[:].rearrange("p mt r -> p (mt r)"), acc[:])
                else:
                    nc.vector.tensor_copy(result[:].rearrange("p mt r -> p (mt r)"), acc[:])
                nc.sync.dma_start(out=out_rows[:, :, first[g] + r0 : first[g] + r0 + n], in_=result[:])

        for step, pc in zip(steps, pieces[6:]):
            squares(*step)
            reciprocals(pc)
        for step in steps[2:2]:
            squares(*step)
        w3_grouped = keep.tile([P, PACK * N], BF16, name="w3_grouped", align_bytes=64)
        nc.vector.tensor_tensor(
            w3_grouped[:].rearrange("p (c i j) -> p c j i", i=4, j=PACK),
            w3_raw[:].rearrange("p j (c i) -> p c j i", i=4),
            unit_sign[:].unsqueeze(1).unsqueeze(3).to_broadcast([P, N // 4, PACK, 4]),
            ALU.mult,
        )
        w3_codes, w3_scales = quantize(w3_grouped, "w3")
        out_rows = out.rearrange("(mt p) r -> p mt r", p=P)

        for i, step in enumerate(steps):
            if i + 2 < len(steps):
                squares(*steps[i + 2])
            amplitude(*step)
            if step[1].stop == PACK:
                finish(step[0])
